import numpy as np
import ml_dtypes


def mxq(x, axis, fmt="e4m3"):
    dtype, down = {"e4m3": (ml_dtypes.float8_e4m3fn, 7), "e5m2": (ml_dtypes.float8_e5m2, 14)}[fmt]
    v = np.moveaxis(np.asarray(x, np.float32).astype(ml_dtypes.bfloat16).astype(np.float64), axis, -1)
    blocks = v.reshape(v.shape[:-1] + (-1, 32))
    amax = np.abs(blocks).max(-1, keepdims=True)
    byte = np.maximum(np.where(amax > 0, np.frexp(amax)[1] - 1 + 127, 0) - down, 1)
    scale = np.exp2(byte - 127.0)
    codes = (blocks / scale).astype(np.float32).astype(dtype).astype(np.float64)
    return np.moveaxis((codes * scale).reshape(v.shape), -1, axis)


WIDE = False


def mx_kscale(k):
    if not WIDE:
        return np.ones(k)
    levels = np.array([10, -10, 5, -5, 0])
    if k % 512:
        return np.exp2(np.random.permutation(np.resize(levels, k // 32))).repeat(32)
    a = np.empty((k // 512, 16))
    for p in range(k // 512):
        a[p, :8] = np.random.permutation(np.resize(levels, 8))
        for g in range(8):
            far = levels[np.abs(levels - a[p, g]) >= 10]
            a[p, g + 8] = far[np.random.randint(len(far))]
    return np.exp2(a.ravel()).repeat(32)


def f64(x):
    return np.asarray(x).astype(np.float64)


def striped8(idx):
    return np.concatenate([v.reshape(-1, 16).T for v in idx]).astype(np.uint16)


def unstriped8(offs):
    return np.stack([offs[16 * g:16 * g + 16].T.reshape(-1) for g in range(8)]).astype(np.int64)


E2M1 = np.array([0.0, 0.5, 1.0, 1.5, 2.0, 3.0, 4.0, 6.0, -0.0, -0.5, -1.0, -1.5, -2.0, -3.0, -4.0, -6.0])


def pack_weight(w, fmt):
    k, n = w.shape
    w = f64(np.asarray(w, np.float32).astype(ml_dtypes.bfloat16)).reshape(k // 32, 32, n)
    amax = np.abs(w).max(1)
    if fmt == "e4m3":
        byte = np.frexp(amax)[1] - 1 + 127 - 7
    else:
        mant, ex = np.frexp(amax / 6.0)
        byte = np.where(mant > 0.5, ex, ex - 1) + 127
    byte = np.clip(np.where(amax > 0, byte, 1), 1, 254)
    scaled = (w * np.exp2(127.0 - byte)[:, None, :]).reshape(k, n).astype(np.float32)
    by_word = np.ascontiguousarray(scaled.reshape(k // 512, 128, 4, n).transpose(0, 1, 3, 2))
    if fmt == "e4m3":
        words = by_word.astype(ml_dtypes.float8_e4m3fn).view(np.uint8)
    else:
        c = by_word.astype(ml_dtypes.float4_e2m1fn).view(np.uint8) & 0xF
        words = (c[..., 0::2] | (c[..., 1::2] << 4)).reshape(k // 512, 128, 2 * n)
    return np.ascontiguousarray(words), np.ascontiguousarray(byte.astype(np.uint8).reshape(k // 512, 16, n))


def unpack_weight(words, scales, fmt):
    g, _, n = scales.shape
    words = np.ascontiguousarray(words).reshape(g, 128, n, -1)
    if fmt == "e4m3":
        vals = words.view(ml_dtypes.float8_e4m3fn).astype(np.float64)
    else:
        nib = np.empty((g, 128, n, 4), np.uint8)
        nib[..., 0::2] = words & 0xF
        nib[..., 1::2] = words >> 4
        vals = E2M1[nib]
    vals = vals * np.repeat(np.exp2(scales.astype(np.float64) - 127.0), 8, axis=1)[..., None]
    return vals.transpose(0, 1, 3, 2).reshape(g * 512, n)


K, M, T, S = 1024, 1024, 2048, 1024


def setup_inputs():
    n = np.random.standard_normal
    s = mx_kscale(K)[:, None]
    u = mx_kscale(512)[:, None]
    p_w4 = pack_weight(n((K, M)) / np.sqrt(K) / s, "e2m1")
    return {
        "x": (n((K, S)) * s).astype(np.float32),
        "w4_words": p_w4[0],
        "w4_scales": p_w4[1],
        "down": (n((K, 512)) / np.sqrt(K) / s * u.T).astype(np.float32),
        "up": (0.5 * n((512, M)) / np.sqrt(512) / u).astype(np.float32),
        "b": (0.3 * n(1024)).astype(np.float32),
        "wgo": np.repeat(np.random.uniform(0.5, 2.0, (8, S)), 16, axis=0).astype(np.float32),
        "offs": striped8(np.stack([np.random.permutation(T)[:S] for _ in range(8)])),
    }


def reference(x, w4_words, w4_scales, down, up, b, wgo, offs):
    x_ = mxq(f64(x), 0, "e4m3")
    w4_ = unpack_weight(w4_words, w4_scales, "e2m1")
    down_ = mxq(f64(down), 0, "e4m3")
    up_ = mxq(f64(up), 0, "e4m3")
    h_ = mxq(down_.T @ x_, 0, "e4m3")
    y = w4_.T @ x_ + up_.T @ h_
    place = unstriped8(offs)[np.arange(M) % 128 // 16]
    out = np.zeros((M, T))
    out[np.arange(M)[:, None], place] = f64(wgo)[np.arange(M) % 128] * (y + f64(b)[:, None])
    return out

@@ -1,0 +1,289 @@
+from contextlib import ExitStack
+
+import concourse.mybir as mybir
+from concourse.masks import make_identity
+
+K, M, T, S, R = 1024, 1024, 2048, 1024, 512
+FLOPS = 2 * S * (K * R + K * M + R * M)
+
+F32 = mybir.dt.float32
+BF16 = mybir.dt.bfloat16
+I32 = mybir.dt.int32
+U32 = mybir.dt.uint32
+U16 = mybir.dt.uint16
+U8 = mybir.dt.uint8
+FP8X4 = mybir.dt.float8_e4m3fn_x4
+FP4X4 = mybir.dt.float4_e2m1fn_x4
+IDENTITY = mybir.ActivationFunctionType.Identity
+MULT = mybir.AluOpType.mult
+
+P = 128
+ROW_TILES = M // P
+
+
+def weave(copy, dst, src):
+    copy(
+        out=dst.rearrange("p (c i t) -> p c t i", i=4, t=4),
+        in_=src.rearrange("p t (c i) -> p c t i", i=4),
+    )
+
+
+def tile_list_hscat_l_bias_kernel(tc, x, w4_words, w4_scales, down, up, b, wgo, offs, out):
+    nc = tc.nc
+    with ExitStack() as ctx:
+        keep = ctx.enter_context(tc.tile_pool(name="keep", bufs=1))
+        hps = ctx.enter_context(tc.psum_pool(name="hps", bufs=4))
+        yps = ctx.enter_context(tc.psum_pool(name="yps", bufs=4))
+
+        def sb(name, width, dtype, tag=None):
+            return keep.tile([P, width], dtype, name=name, tag=tag or name, align_bytes=64)
+
+        def quantize(codes, scales, values):
+            nc.vector.quantize_mx(out=codes.bitcast(FP8X4), scales=scales, in_=values)
+
+        w4_sc = sb("w4_sc", 2 * M, U8)
+        nc.gpsimd.memset(w4_sc[:].bitcast(I32), 0)
+        for q in range(4):
+            nc.gpsimd.dma_start(
+                out=w4_sc[32 * q : 32 * q + 4, :].bitcast(I32).rearrange("r (a n) -> r a n", a=2),
+                in_=w4_scales[:, 4 * q : 4 * q + 4, :].bitcast(I32).rearrange("a r n -> r a n"),
+            )
+        b_rows = sb("b_rows", P, F32)
+        nc.gpsimd.memset(b_rows[:], 0.0)
+        nc.gpsimd.dma_start(out=b_rows[0:ROW_TILES, :], in_=b.rearrange("(i p) -> i p", p=P))
+        ident = sb("ident", P, F32)
+        make_identity(nc, ident[:])
+
+        def load_rows(name, src, a, c0, w):
+            raw = sb(name, 4 * w, F32)
+            nc.sync.dma_start(
+                out=raw[:].rearrange("p (j c) -> p j c", j=4),
+                in_=src[512 * a : 512 * (a + 1), c0 : c0 + w].rearrange("(p j) c -> p j c", j=4),
+            )
+            return raw
+
+        def load_w4(name, half):
+            words = sb(name, 2 * M, U8)
+            nc.sync.dma_start(
+                out=words[:].bitcast(I32).rearrange("p (a n) -> p a n", a=2),
+                in_=w4_words[:, :, M * half : M * (half + 1)].bitcast(I32).rearrange("a p n -> p a n"),
+            )
+            return words
+
+        d_raw = [None, None]
+        x_raw = [[None, None] for c in range(3)]
+        d_raw[0] = load_rows("d_raw0", down, 0, 0, R)
+        x_raw[0][0] = load_rows("x_raw00", x, 0, 0, 256)
+        d_raw[1] = load_rows("d_raw1", down, 1, 0, R)
+        x_raw[0][1] = load_rows("x_raw01", x, 1, 0, 256)
+        upa_raw = load_rows("upa_raw", up, 0, 0, 256)
+        w4_lo = load_w4("w4_lo", 0)
+        wg_lo = sb("wg_lo", 256, F32)
+        nc.sync.dma_start(out=wg_lo[:], in_=wgo[:, 0:256])
+        offsets = keep.tile([P, S // 16], U16, name="offsets")
+        nc.sync.dma_start(offsets[:], offs)
+        upb_raw = load_rows("upb_raw", up, 0, 256, 256)
+        upc_raw = load_rows("upc_raw", up, 0, 512, 512)
+        w4_hi = load_w4("w4_hi", 1)
+        x_raw[1][0] = load_rows("x_raw10", x, 0, 256, 256)
+        x_raw[1][1] = load_rows("x_raw11", x, 1, 256, 256)
+        wg_hi = sb("wg_hi", 768, F32)
+        nc.sync.dma_start(out=wg_hi[:], in_=wgo[:, 256:S])
+        x_raw[2][0] = load_rows("x_raw20", x, 0, 512, 512)
+        x_raw[2][1] = load_rows("x_raw21", x, 1, 512, 512)
+
+        def rows4(raw, c0, w):
+            return raw[:].rearrange("p (j c) -> p j c", j=4)[:, :, c0 : c0 + w]
+
+        b_ps = yps.tile([P, 512], F32, name="y_ps", tag="y_ps")
+        nc.tensor.transpose(b_ps[:, 0:P], b_rows[:], ident[:])
+        b_col = sb("b_col", ROW_TILES, F32)
+        nc.scalar.activation(out=b_col[:], in_=b_ps[:, 0:ROW_TILES], func=IDENTITY)
+
+        d_codes = [sb("d_codes%d" % a, R, U32) for a in range(2)]
+        d_sc = [sb("d_sc%d" % a, R, U8) for a in range(2)]
+        up_codes = sb("up_codes", M, U32)
+        up_sc = sb("up_sc", M, U8)
+        widths = [256, 256, 512]
+        starts = [0, 256, 512]
+        x_codes = [[sb("x_codes%d%d" % (c, a), widths[c], U32) for a in range(2)] for c in (0, 2)]
+        x1_codes = sb("x1_codes", 512, U32)
+        x_codes = [[t[:] for t in x_codes[0]], [x1_codes[:, 0:256], x1_codes[:, 256:512]], [t[:] for t in x_codes[1]]]
+        x0_sc = [sb("x0_sc%d" % a, 256, U8) for a in range(2)]
+        x1_sc = sb("x1_sc", 512, U8)
+        x2_sc = [sb("x2_sc%d" % a, 512, U8) for a in range(2)]
+        x_sc = [[t[:] for t in x0_sc], [x1_sc[:, 0:256], x1_sc[:, 256:512]], [t[:] for t in x2_sc]]
+        h_codes = [sb("h_codes%d" % c, widths[c], U32) for c in range(3)]
+        h2_sc = sb("h2_sc", 512, U8)
+        h_sc = [x1_sc[4:P, 0:256], x2_sc[1][4:P, 0:256], h2_sc[:]]
+
+        def down_pass(a):
+            raw = d_raw[a][:].rearrange("p (j m t) -> p m j t", j=4, t=4)
+            for half, copy in enumerate((nc.vector.tensor_copy, nc.scalar.copy)):
+                rounded = sb("d_bf%d%d" % (a, half), 1024, BF16)
+                copy(
+                    out=rounded[:].rearrange("p (t m j) -> p m j t", t=2, j=4),
+                    in_=raw[:, :, :, 2 * half : 2 * half + 2],
+                )
+                cols = slice(256 * half, 256 * (half + 1))
+                quantize(d_codes[a][:, cols], d_sc[a][:, cols], rounded[:])
+
+        def x0_pass(a):
+            for half, copy in enumerate((nc.vector.tensor_copy, nc.scalar.copy)):
+                rounded = sb("x0_bf%d%d" % (a, half), 512, BF16)
+                weave(copy, rounded[:], rows4(x_raw[0][a], P * half, P))
+                cols = slice(P * half, P * (half + 1))
+                quantize(x_codes[0][a][:, cols], x_sc[0][a][:, cols], rounded[:])
+
+        def scalar_weave(rounded, raw, w):
+            for c0 in range(0, w, P):
+                weave(nc.scalar.copy, rounded[:, 4 * c0 : 4 * (c0 + P)], rows4(raw, c0, P))
+
+        def h_pass(c, a, banks):
+            for i, bank in enumerate(banks):
+                cols = slice(P * i, P * (i + 1))
+                for t in range(4):
+                    m_cols = slice(P * t, P * (t + 1))
+                    nc.tensor.matmul_mx(
+                        out=bank[:, m_cols],
+                        lhsT=d_codes[a][:, m_cols].bitcast(FP8X4),
+                        lhsT_scale=d_sc[a][:, m_cols],
+                        rhs=x_codes[c][a][:, cols].bitcast(FP8X4),
+                        rhs_scale=x_sc[c][a][:, cols],
+                        start=(a == 0 and t == 0),
+                        stop=(a == 1 and t == 3),
+                    )
+
+        def h_banks(c):
+            return [hps.tile([P, 512], F32, name="h_ps", tag="h_ps") for i in range(widths[c] // P)]
+
+        def h_out(copy, rounded, i, bank):
+            copy(
+                out=rounded[:, 512 * i : 512 * (i + 1)].rearrange("p (n t) -> p n t", t=4),
+                in_=bank[:].rearrange("p (t n) -> p n t", t=4),
+            )
+
+        def y_sum(c, r):
+            w = widths[c]
+            n = P if w < 512 else w
+            bank = yps.tile([P, 512], F32, name="y_ps", tag="y_ps")
+            words = w4_lo if r < 4 else w4_hi
+            for a in range(2):
+                w0 = M * a + 256 * (r % 4)
+                s0 = M * a + P * r
+                for c0 in range(0, w, n):
+                    nc.tensor.matmul_mx(
+                        out=bank[:, c0 : c0 + n],
+                        lhsT=words[:, w0 : w0 + 256].bitcast(FP4X4),
+                        lhsT_scale=w4_sc[:, s0 : s0 + P],
+                        rhs=x_codes[c][a][:, c0 : c0 + n].bitcast(FP8X4),
+                        rhs_scale=x_sc[c][a][:, c0 : c0 + n],
+                        start=(a == 0 and c0 == 0),
+                        stop=False,
+                    )
+            m_cols = slice(P * r, P * (r + 1))
+            nc.tensor.matmul_mx(
+                out=bank[:, 0:w],
+                lhsT=up_codes[:, m_cols].bitcast(FP8X4),
+                lhsT_scale=up_sc[:, m_cols],
+                rhs=h_codes[c][:].bitcast(FP8X4),
+                rhs_scale=h_sc[c],
+                start=False,
+                stop=True,
+            )
+            return bank
+
+        pages = [None] * ROW_TILES
+
+        def clear(memset, r, tag=None):
+            pages[r] = sb("page%d" % r, T, F32, tag)
+            memset(pages[r][:], 0.0)
+
+        def place(c, r, bank, staged):
+            w, c0 = widths[c], starts[c]
+            nc.scalar.activation(out=staged, in_=bank[:, 0:w], func=IDENTITY, bias=b_col[:, r : r + 1])
+            weights = wg_lo[:] if c == 0 else wg_hi[:, c0 - 256 : c0 - 256 + w]
+            nc.vector.tensor_tensor(
+                pages[r][:].indirect(offsets[:, c0 // 16 : (c0 + w) // 16]), staged, weights, MULT
+            )
+            if c == 2:
+                nc.sync.dma_start(out=out[P * r : P * (r + 1), :], in_=pages[r][:])
+
+        def slot(raw, i, w):
+            return raw[:, w * i : w * (i + 1)]
+
+        def last(raw, w, i):
+            return raw[:, w * (i + 1) - 256 : w * (i + 1)]
+
+        banks = h_banks(0)
+        down_pass(0)
+        x0_pass(0)
+        h_pass(0, 0, banks)
+        down_pass(1)
+        x0_pass(1)
+        h_pass(0, 1, banks)
+        h0_bf = sb("h0_bf", 1024, BF16, "late4")
+        upa_bf = sb("upa_bf", 1024, BF16)
+        for half, copy in enumerate((nc.vector.tensor_copy, nc.scalar.copy)):
+            cols = slice(P * half, P * (half + 1))
+            wide = slice(512 * half, 512 * (half + 1))
+            h_out(copy, h0_bf, half, banks[half])
+            quantize(h_codes[0][:, cols], h_sc[0][:, cols], h0_bf[:, wide])
+            weave(copy, upa_bf[:, wide], rows4(upa_raw, P * half, P))
+            quantize(up_codes[:, cols], up_sc[:, cols], upa_bf[:, wide])
+        for r in range(4):
+            clear(nc.vector.memset, r)
+        clear(nc.gpsimd.memset, 4, "late4")
+
+        place(0, 0, y_sum(0, 0), slot(d_raw[0], 0, 256))
+        upb_bf = sb("upb_bf", 1024, BF16, "late5")
+        scalar_weave(upb_bf, upb_raw, 256)
+        quantize(up_codes[:, 256:512], up_sc[:, 256:512], upb_bf[:])
+        clear(nc.gpsimd.memset, 5, "late5")
+        place(0, 1, y_sum(0, 1), last(upb_raw, 256, 0))
+        place(0, 2, y_sum(0, 2), slot(d_raw[0], 1, 256))
+        upc_bf = sb("upc_bf", 2048, BF16, "late6")
+        scalar_weave(upc_bf, upc_raw, 512)
+        quantize(up_codes[:, 512:M], up_sc[:, 512:M], upc_bf[:])
+        clear(nc.gpsimd.memset, 6, "late6")
+        place(0, 3, y_sum(0, 3), last(upc_raw, 512, 0))
+        place(0, 4, y_sum(0, 4), slot(d_raw[0], 2, 256))
+        held = [y_sum(0, r) for r in (5, 6)]
+        x1_bf = sb("x1_bf", 2048, BF16, "late7")
+        for a in range(2):
+            scalar_weave(x1_bf[:, 1024 * a : 1024 * (a + 1)], x_raw[1][a], 256)
+        quantize(x1_codes[:], x1_sc[:], x1_bf[:])
+        clear(nc.gpsimd.memset, 7, "late7")
+        banks = h_banks(1)
+        h_pass(1, 0, banks)
+        h_pass(1, 1, banks)
+        for i, r in enumerate((5, 6)):
+            place(0, r, held[i], last(x_raw[1][1], 256, i))
+        h1_bf = sb("h1_bf", 1024, BF16)
+        for i in range(2):
+            h_out(nc.scalar.copy, h1_bf, i, banks[i])
+        quantize(h_codes[1][:], h_sc[1], h1_bf[:])
+        place(0, 7, y_sum(0, 7), slot(d_raw[0], 3, 256))
+
+        for r in (0, 1):
+            place(1, r, y_sum(1, r), slot(d_raw[0], 4 + r, 256))
+        banks = h_banks(2)
+        for a in range(2):
+            rows = (2 + 2 * a, 3 + 2 * a)
+            held = [y_sum(1, r) for r in rows]
+            x2_bf = sb("x2_bf%d" % a, 2048, BF16)
+            scalar_weave(x2_bf, x_raw[2][a], 512)
+            quantize(x_codes[2][a], x_sc[2][a], x2_bf[:])
+            h_pass(2, a, banks)
+            for i, r in enumerate(rows):
+                place(1, r, held[i], last(x_raw[2][a], 512, i))
+        h2_bf = sb("h2_bf", 2048, BF16)
+        for i in range(4):
+            h_out(nc.scalar.copy, h2_bf, i, banks[i])
+        quantize(h_codes[2][:], h_sc[2], h2_bf[:])
+        for r in (6, 7):
+            place(1, r, y_sum(1, r), slot(d_raw[0], r, 256))
+
+        spare = [d_raw[1], upc_raw]
+        for r in range(ROW_TILES):
+            place(2, r, y_sum(2, r), slot(spare[r // 4], r % 4, 512))

@@ -19,6 +19,9 @@ MULT = mybir.AluOpType.mult
 
 P = 128
 ROW_TILES = M // P
+PAGES = 5
+CHUNK = 256
+CHUNKS = S // CHUNK
 
 
 def weave(copy, dst, src):
@@ -35,24 +38,30 @@ def tile_list_hscat_l_bias_kernel(tc, x, w4_words, w4_scales, down, up, b, wgo, 
         hps = ctx.enter_context(tc.psum_pool(name="hps", bufs=4))
         yps = ctx.enter_context(tc.psum_pool(name="yps", bufs=4))
 
-        def sb(name, width, dtype, tag=None):
-            return keep.tile([P, width], dtype, name=name, tag=tag or name, align_bytes=64)
+        def sb(name, width, dtype):
+            return keep.tile([P, width], dtype, name=name, align_bytes=64)
 
         def quantize(codes, scales, values):
             nc.vector.quantize_mx(out=codes.bitcast(FP8X4), scales=scales, in_=values)
 
-        w4_sc = sb("w4_sc", 2 * M, U8)
-        nc.gpsimd.memset(w4_sc[:].bitcast(I32), 0)
-        for q in range(4):
-            nc.gpsimd.dma_start(
-                out=w4_sc[32 * q : 32 * q + 4, :].bitcast(I32).rearrange("r (a n) -> r a n", a=2),
-                in_=w4_scales[:, 4 * q : 4 * q + 4, :].bitcast(I32).rearrange("a r n -> r a n"),
-            )
         b_rows = sb("b_rows", P, F32)
         nc.gpsimd.memset(b_rows[:], 0.0)
         nc.gpsimd.dma_start(out=b_rows[0:ROW_TILES, :], in_=b.rearrange("(i p) -> i p", p=P))
         ident = sb("ident", P, F32)
         make_identity(nc, ident[:])
+        w4_sc = sb("w4_sc", 2 * M, U8)
+        nc.vector.memset(w4_sc[:].bitcast(I32), 0)
+        for q in range(4):
+            nc.gpsimd.dma_start(
+                out=w4_sc[32 * q : 32 * q + 4, :].bitcast(I32).rearrange("r (a n) -> r a n", a=2),
+                in_=w4_scales[:, 4 * q : 4 * q + 4, :].bitcast(I32).rearrange("a r n -> r a n"),
+            )
+        pages = [sb("page%d" % r, T, F32) for r in range(PAGES)]
+        for r in range(2):
+            for cols in (slice(0, 1023), slice(1023, T)):
+                nc.vector.memset(pages[r][:, cols], 0.0)
+        for cols in (slice(0, 1024), slice(1024, T)):
+            nc.gpsimd.memset(pages[2][:, cols], 0.0)
 
         def load_rows(name, src, a, c0, w):
             raw = sb(name, 4 * w, F32)
@@ -62,35 +71,36 @@ def tile_list_hscat_l_bias_kernel(tc, x, w4_words, w4_scales, down, up, b, wgo, 
             )
             return raw
 
-        def load_w4(name, half):
-            words = sb(name, 2 * M, U8)
+        def load_w4(name, r0, r1):
+            words = sb(name, 512 * (r1 - r0), U8)
             nc.sync.dma_start(
                 out=words[:].bitcast(I32).rearrange("p (a n) -> p a n", a=2),
-                in_=w4_words[:, :, M * half : M * (half + 1)].bitcast(I32).rearrange("a p n -> p a n"),
+                in_=w4_words[:, :, 256 * r0 : 256 * r1].bitcast(I32).rearrange("a p n -> p a n"),
             )
             return words
 
-        d_raw = [None, None]
-        x_raw = [[None, None] for c in range(3)]
-        d_raw[0] = load_rows("d_raw0", down, 0, 0, R)
-        x_raw[0][0] = load_rows("x_raw00", x, 0, 0, 256)
-        d_raw[1] = load_rows("d_raw1", down, 1, 0, R)
-        x_raw[0][1] = load_rows("x_raw01", x, 1, 0, 256)
-        upa_raw = load_rows("upa_raw", up, 0, 0, 256)
-        w4_lo = load_w4("w4_lo", 0)
-        wg_lo = sb("wg_lo", 256, F32)
-        nc.sync.dma_start(out=wg_lo[:], in_=wgo[:, 0:256])
+        def load_x(c, a):
+            return load_rows("x_raw%d%d" % (c, a), x, a, CHUNK * c, CHUNK)
+
+        d_raw = []
+        x_raw = [[] for c in range(CHUNKS)]
+        for a in range(2):
+            d_raw.append(load_rows("d_raw%d" % a, down, a, 0, R))
+            x_raw[0].append(load_x(0, a))
+        upa_raw = load_rows("upa_raw", up, 0, 0, 2 * P)
+        w4_lo = load_w4("w4_lo", 0, PAGES)
+        wg = sb("wg", S, F32)
+        nc.sync.dma_start(out=wg[:, 0:CHUNK], in_=wgo[:, 0:CHUNK])
         offsets = keep.tile([P, S // 16], U16, name="offsets")
         nc.sync.dma_start(offsets[:], offs)
-        upb_raw = load_rows("upb_raw", up, 0, 256, 256)
-        upc_raw = load_rows("upc_raw", up, 0, 512, 512)
-        w4_hi = load_w4("w4_hi", 1)
-        x_raw[1][0] = load_rows("x_raw10", x, 0, 256, 256)
-        x_raw[1][1] = load_rows("x_raw11", x, 1, 256, 256)
-        wg_hi = sb("wg_hi", 768, F32)
-        nc.sync.dma_start(out=wg_hi[:], in_=wgo[:, 256:S])
-        x_raw[2][0] = load_rows("x_raw20", x, 0, 512, 512)
-        x_raw[2][1] = load_rows("x_raw21", x, 1, 512, 512)
+        upb_raw = load_rows("upb_raw", up, 0, 2 * P, (PAGES - 2) * P)
+        for c in range(1, CHUNKS):
+            for a in range(2):
+                x_raw[c].append(load_x(c, a))
+            if c == 1:
+                nc.sync.dma_start(out=wg[:, CHUNK:S], in_=wgo[:, CHUNK:S])
+        upc_raw = load_rows("upc_raw", up, 0, PAGES * P, M - PAGES * P)
+        w4_hi = load_w4("w4_hi", PAGES, ROW_TILES)
 
         def rows4(raw, c0, w):
             return raw[:].rearrange("p (j c) -> p j c", j=4)[:, :, c0 : c0 + w]
@@ -104,18 +114,10 @@ def tile_list_hscat_l_bias_kernel(tc, x, w4_words, w4_scales, down, up, b, wgo, 
         d_sc = [sb("d_sc%d" % a, R, U8) for a in range(2)]
         up_codes = sb("up_codes", M, U32)
         up_sc = sb("up_sc", M, U8)
-        widths = [256, 256, 512]
-        starts = [0, 256, 512]
-        x_codes = [[sb("x_codes%d%d" % (c, a), widths[c], U32) for a in range(2)] for c in (0, 2)]
-        x1_codes = sb("x1_codes", 512, U32)
-        x_codes = [[t[:] for t in x_codes[0]], [x1_codes[:, 0:256], x1_codes[:, 256:512]], [t[:] for t in x_codes[1]]]
-        x0_sc = [sb("x0_sc%d" % a, 256, U8) for a in range(2)]
-        x1_sc = sb("x1_sc", 512, U8)
-        x2_sc = [sb("x2_sc%d" % a, 512, U8) for a in range(2)]
-        x_sc = [[t[:] for t in x0_sc], [x1_sc[:, 0:256], x1_sc[:, 256:512]], [t[:] for t in x2_sc]]
-        h_codes = [sb("h_codes%d" % c, widths[c], U32) for c in range(3)]
-        h2_sc = sb("h2_sc", 512, U8)
-        h_sc = [x1_sc[4:P, 0:256], x2_sc[1][4:P, 0:256], h2_sc[:]]
+        x_codes = [sb("x_codes%d" % a, S, U32) for a in range(2)]
+        x_sc = [sb("x_sc0", S, U8), sb("x_sc1", S + CHUNK, U8)]
+        h_codes = sb("h_codes", S, U32)
+        h_sc = x_sc[1][4:P, CHUNK : S + CHUNK]
 
         def down_pass(a):
             raw = d_raw[a][:].rearrange("p (j m t) -> p m j t", j=4, t=4)
@@ -133,29 +135,37 @@ def tile_list_hscat_l_bias_kernel(tc, x, w4_words, w4_scales, down, up, b, wgo, 
                 rounded = sb("x0_bf%d%d" % (a, half), 512, BF16)
                 weave(copy, rounded[:], rows4(x_raw[0][a], P * half, P))
                 cols = slice(P * half, P * (half + 1))
-                quantize(x_codes[0][a][:, cols], x_sc[0][a][:, cols], rounded[:])
+                quantize(x_codes[a][:, cols], x_sc[a][:, cols], rounded[:])
 
-        def scalar_weave(rounded, raw, w):
+        def scalar_weave(name, raw, w):
+            rounded = sb(name, 4 * w, BF16)
             for c0 in range(0, w, P):
                 weave(nc.scalar.copy, rounded[:, 4 * c0 : 4 * (c0 + P)], rows4(raw, c0, P))
+            return rounded
+
+        def up_rows(name, raw, r0, r1):
+            rounded = scalar_weave(name, raw, P * (r1 - r0))
+            for i0, i1 in ((0, 2), (2, 3)):
+                cols = slice(P * (r0 + i0), P * (r0 + i1))
+                quantize(up_codes[:, cols], up_sc[:, cols], rounded[:, 512 * i0 : 512 * i1])
 
         def h_pass(c, a, banks):
             for i, bank in enumerate(banks):
-                cols = slice(P * i, P * (i + 1))
+                cols = slice(CHUNK * c + P * i, CHUNK * c + P * (i + 1))
                 for t in range(4):
                     m_cols = slice(P * t, P * (t + 1))
                     nc.tensor.matmul_mx(
                         out=bank[:, m_cols],
                         lhsT=d_codes[a][:, m_cols].bitcast(FP8X4),
                         lhsT_scale=d_sc[a][:, m_cols],
-                        rhs=x_codes[c][a][:, cols].bitcast(FP8X4),
-                        rhs_scale=x_sc[c][a][:, cols],
+                        rhs=x_codes[a][:, cols].bitcast(FP8X4),
+                        rhs_scale=x_sc[a][:, cols],
                         start=(a == 0 and t == 0),
                         stop=(a == 1 and t == 3),
                     )
 
-        def h_banks(c):
-            return [hps.tile([P, 512], F32, name="h_ps", tag="h_ps") for i in range(widths[c] // P)]
+        def h_banks():
+            return [hps.tile([P, 512], F32, name="h_ps", tag="h_ps") for i in range(CHUNK // P)]
 
         def h_out(copy, rounded, i, bank):
             copy(
@@ -163,22 +173,22 @@ def tile_list_hscat_l_bias_kernel(tc, x, w4_words, w4_scales, down, up, b, wgo, 
                 in_=bank[:].rearrange("p (t n) -> p n t", t=4),
             )
 
-        def y_sum(c, r):
-            w = widths[c]
+        def y_sum(r, c0, w):
             n = P if w < 512 else w
             bank = yps.tile([P, 512], F32, name="y_ps", tag="y_ps")
-            words = w4_lo if r < 4 else w4_hi
+            words, i, count = (w4_lo, r, PAGES) if r < PAGES else (w4_hi, r - PAGES, ROW_TILES - PAGES)
             for a in range(2):
-                w0 = M * a + 256 * (r % 4)
+                w0 = 256 * (count * a + i)
                 s0 = M * a + P * r
-                for c0 in range(0, w, n):
+                for j in range(0, w, n):
+                    cols = slice(c0 + j, c0 + j + n)
                     nc.tensor.matmul_mx(
-                        out=bank[:, c0 : c0 + n],
+                        out=bank[:, j : j + n],
                         lhsT=words[:, w0 : w0 + 256].bitcast(FP4X4),
                         lhsT_scale=w4_sc[:, s0 : s0 + P],
-                        rhs=x_codes[c][a][:, c0 : c0 + n].bitcast(FP8X4),
-                        rhs_scale=x_sc[c][a][:, c0 : c0 + n],
-                        start=(a == 0 and c0 == 0),
+                        rhs=x_codes[a][:, cols].bitcast(FP8X4),
+                        rhs_scale=x_sc[a][:, cols],
+                        start=(a == 0 and j == 0),
                         stop=False,
                     )
             m_cols = slice(P * r, P * (r + 1))
@@ -186,104 +196,86 @@ def tile_list_hscat_l_bias_kernel(tc, x, w4_words, w4_scales, down, up, b, wgo, 
                 out=bank[:, 0:w],
                 lhsT=up_codes[:, m_cols].bitcast(FP8X4),
                 lhsT_scale=up_sc[:, m_cols],
-                rhs=h_codes[c][:].bitcast(FP8X4),
-                rhs_scale=h_sc[c],
+                rhs=h_codes[:, c0 : c0 + w].bitcast(FP8X4),
+                rhs_scale=h_sc[:, c0 : c0 + w],
                 start=False,
                 stop=True,
             )
-            return bank
+            return bank[:, 0:w]
 
-        pages = [None] * ROW_TILES
+        def add_bias(r, staged, bank):
+            nc.scalar.activation(out=staged, in_=bank, func=IDENTITY, bias=b_col[:, r : r + 1])
 
-        def clear(memset, r, tag=None):
-            pages[r] = sb("page%d" % r, T, F32, tag)
-            memset(pages[r][:], 0.0)
+        def scatter(r, c0, w, staged):
+            page = pages[r % PAGES]
+            nc.vector.tensor_tensor(
+                page[:].indirect(offsets[:, c0 // 16 : (c0 + w) // 16]), staged, wg[:, c0 : c0 + w], MULT
+            )
+            if c0 + w == S:
+                nc.sync.dma_start(out=out[P * r : P * (r + 1), :], in_=page[:])
 
         def place(c, r, bank, staged):
-            w, c0 = widths[c], starts[c]
-            nc.scalar.activation(out=staged, in_=bank[:, 0:w], func=IDENTITY, bias=b_col[:, r : r + 1])
-            weights = wg_lo[:] if c == 0 else wg_hi[:, c0 - 256 : c0 - 256 + w]
-            nc.vector.tensor_tensor(
-                pages[r][:].indirect(offsets[:, c0 // 16 : (c0 + w) // 16]), staged, weights, MULT
-            )
-            if c == 2:
-                nc.sync.dma_start(out=out[P * r : P * (r + 1), :], in_=pages[r][:])
-
-        def slot(raw, i, w):
-            return raw[:, w * i : w * (i + 1)]
+            add_bias(r, staged, bank)
+            scatter(r, CHUNK * c, CHUNK, staged)
 
         def last(raw, w, i):
-            return raw[:, w * (i + 1) - 256 : w * (i + 1)]
+            return raw[:, w * (i + 1) - CHUNK : w * (i + 1)]
 
-        banks = h_banks(0)
-        down_pass(0)
-        x0_pass(0)
-        h_pass(0, 0, banks)
-        down_pass(1)
-        x0_pass(1)
-        h_pass(0, 1, banks)
-        h0_bf = sb("h0_bf", 1024, BF16, "late4")
+        staging = sb("staging", 3 * CHUNKS * CHUNK, F32)
+
+        def free(c, i):
+            return staging[:, CHUNK * (3 * c + i) : CHUNK * (3 * c + i + 1)]
+
+        banks = h_banks()
+        for a in range(2):
+            down_pass(a)
+            x0_pass(a)
+            h_pass(0, a, banks)
+        h_bf = sb("h_bf0", 1024, BF16)
         upa_bf = sb("upa_bf", 1024, BF16)
         for half, copy in enumerate((nc.vector.tensor_copy, nc.scalar.copy)):
             cols = slice(P * half, P * (half + 1))
             wide = slice(512 * half, 512 * (half + 1))
-            h_out(copy, h0_bf, half, banks[half])
-            quantize(h_codes[0][:, cols], h_sc[0][:, cols], h0_bf[:, wide])
+            h_out(copy, h_bf, half, banks[half])
+            quantize(h_codes[:, cols], h_sc[:, cols], h_bf[:, wide])
             weave(copy, upa_bf[:, wide], rows4(upa_raw, P * half, P))
             quantize(up_codes[:, cols], up_sc[:, cols], upa_bf[:, wide])
-        for r in range(4):
-            clear(nc.vector.memset, r)
-        clear(nc.gpsimd.memset, 4, "late4")
+            add_bias(0, free(0, 0)[:, cols], y_sum(0, P * half, P))
+            scatter(0, P * half, P, free(0, 0)[:, cols])
+        for r in range(3, PAGES):
+            for half in range(2):
+                nc.vector.memset(pages[r][:, 1024 * half : 1024 * (half + 1)], 0.0)
 
-        place(0, 0, y_sum(0, 0), slot(d_raw[0], 0, 256))
-        upb_bf = sb("upb_bf", 1024, BF16, "late5")
-        scalar_weave(upb_bf, upb_raw, 256)
-        quantize(up_codes[:, 256:512], up_sc[:, 256:512], upb_bf[:])
-        clear(nc.gpsimd.memset, 5, "late5")
-        place(0, 1, y_sum(0, 1), last(upb_raw, 256, 0))
-        place(0, 2, y_sum(0, 2), slot(d_raw[0], 1, 256))
-        upc_bf = sb("upc_bf", 2048, BF16, "late6")
-        scalar_weave(upc_bf, upc_raw, 512)
-        quantize(up_codes[:, 512:M], up_sc[:, 512:M], upc_bf[:])
-        clear(nc.gpsimd.memset, 6, "late6")
-        place(0, 3, y_sum(0, 3), last(upc_raw, 512, 0))
-        place(0, 4, y_sum(0, 4), slot(d_raw[0], 2, 256))
-        held = [y_sum(0, r) for r in (5, 6)]
-        x1_bf = sb("x1_bf", 2048, BF16, "late7")
-        for a in range(2):
-            scalar_weave(x1_bf[:, 1024 * a : 1024 * (a + 1)], x_raw[1][a], 256)
-        quantize(x1_codes[:], x1_sc[:], x1_bf[:])
-        clear(nc.gpsimd.memset, 7, "late7")
-        banks = h_banks(1)
-        h_pass(1, 0, banks)
-        h_pass(1, 1, banks)
-        for i, r in enumerate((5, 6)):
-            place(0, r, held[i], last(x_raw[1][1], 256, i))
-        h1_bf = sb("h1_bf", 1024, BF16)
-        for i in range(2):
-            h_out(nc.scalar.copy, h1_bf, i, banks[i])
-        quantize(h_codes[1][:], h_sc[1], h1_bf[:])
-        place(0, 7, y_sum(0, 7), slot(d_raw[0], 3, 256))
+        for c in range(CHUNKS):
+            c0 = CHUNK * c
+            if c == 0:
+                up_rows("upb_bf", upb_raw, 2, PAGES)
+            else:
+                place(c, 0, y_sum(0, c0, CHUNK), free(c, 0))
+            place(c, 1, y_sum(1, c0, CHUNK), last(upb_raw, 3 * P, 0) if c == 0 else free(c, 1))
+            held = [y_sum(r, c0, CHUNK) for r in (2, 3)]
+            if c + 1 < CHUNKS:
+                cols = slice(c0 + CHUNK, c0 + 2 * CHUNK)
+                banks = h_banks()
+                for a in range(2):
+                    x_bf = scalar_weave("x_bf%d%d" % (c + 1, a), x_raw[c + 1][a], CHUNK)
+                    quantize(x_codes[a][:, cols], x_sc[a][:, cols], x_bf[:])
+                    h_pass(c + 1, a, banks)
+                for i in range(2):
+                    place(c, 2 + i, held[i], last(x_raw[c + 1][1], CHUNK, i))
+                h_bf = sb("h_bf%d" % (c + 1), 1024, BF16)
+                for i in range(2):
+                    h_out(nc.scalar.copy, h_bf, i, banks[i])
+                quantize(h_codes[:, cols], h_sc[:, cols], h_bf[:])
+            else:
+                up_rows("upc_bf", upc_raw, PAGES, ROW_TILES)
+                for i in range(2):
+                    place(c, 2 + i, held[i], last(upc_raw, 3 * P, i))
+            place(c, 4, y_sum(4, c0, CHUNK), free(c, 2))
 
-        for r in (0, 1):
-            place(1, r, y_sum(1, r), slot(d_raw[0], 4 + r, 256))
-        banks = h_banks(2)
-        for a in range(2):
-            rows = (2 + 2 * a, 3 + 2 * a)
-            held = [y_sum(1, r) for r in rows]
-            x2_bf = sb("x2_bf%d" % a, 2048, BF16)
-            scalar_weave(x2_bf, x_raw[2][a], 512)
-            quantize(x_codes[2][a], x_sc[2][a], x2_bf[:])
-            h_pass(2, a, banks)
-            for i, r in enumerate(rows):
-                place(1, r, held[i], last(x_raw[2][a], 512, i))
-        h2_bf = sb("h2_bf", 2048, BF16)
-        for i in range(4):
-            h_out(nc.scalar.copy, h2_bf, i, banks[i])
-        quantize(h_codes[2][:], h_sc[2], h2_bf[:])
-        for r in (6, 7):
-            place(1, r, y_sum(1, r), slot(d_raw[0], r, 256))
-
-        spare = [d_raw[1], upc_raw]
-        for r in range(ROW_TILES):
-            place(2, r, y_sum(2, r), slot(spare[r // 4], r % 4, 512))
+        spare = [d_raw[0][:, 0:S], d_raw[0][:, S : 2 * S], d_raw[1][:, 0:S]]
+        for r in range(PAGES, ROW_TILES):
+            staged = spare[r - PAGES]
+            for c0 in range(0, S, 512):
+                add_bias(r, staged[:, c0 : c0 + 512], y_sum(r, c0, 512))
+            scatter(r, 0, S, staged)

@@ -18,10 +18,13 @@ IDENTITY = mybir.ActivationFunctionType.Identity
 MULT = mybir.AluOpType.mult
 
 P = 128
+PASS = 4 * P
+BANK = 512
 ROW_TILES = M // P
-PAGES = 5
 CHUNK = 256
 CHUNKS = S // CHUNK
+PAGES = 5
+W4_FIRST = 4
 
 
 def weave(copy, dst, src):
@@ -35,11 +38,11 @@ def tile_list_hscat_l_bias_kernel(tc, x, w4_words, w4_scales, down, up, b, wgo, 
     nc = tc.nc
     with ExitStack() as ctx:
         keep = ctx.enter_context(tc.tile_pool(name="keep", bufs=1))
-        hps = ctx.enter_context(tc.psum_pool(name="hps", bufs=4))
-        yps = ctx.enter_context(tc.psum_pool(name="yps", bufs=4))
+        h_psum = ctx.enter_context(tc.psum_pool(name="h_psum", bufs=4))
+        y_psum = ctx.enter_context(tc.psum_pool(name="y_psum", bufs=4))
 
-        def sb(name, width, dtype):
-            return keep.tile([P, width], dtype, name=name, align_bytes=64)
+        def sb(name, width, dtype, tag=None):
+            return keep.tile([P, width], dtype, name=name, tag=tag or name, align_bytes=64)
 
         def quantize(codes, scales, values):
             nc.vector.quantize_mx(out=codes.bitcast(FP8X4), scales=scales, in_=values)
@@ -56,62 +59,68 @@ def tile_list_hscat_l_bias_kernel(tc, x, w4_words, w4_scales, down, up, b, wgo, 
                 out=w4_sc[32 * q : 32 * q + 4, :].bitcast(I32).rearrange("r (a n) -> r a n", a=2),
                 in_=w4_scales[:, 4 * q : 4 * q + 4, :].bitcast(I32).rearrange("a r n -> r a n"),
             )
-        pages = [sb("page%d" % r, T, F32) for r in range(PAGES)]
-        for r in range(2):
-            for cols in (slice(0, 1023), slice(1023, T)):
-                nc.vector.memset(pages[r][:, cols], 0.0)
-        for cols in (slice(0, 1024), slice(1024, T)):
-            nc.gpsimd.memset(pages[2][:, cols], 0.0)
+
+        pages = [sb("page%d" % r, T, F32) for r in range(2)]
+        for page in pages:
+            nc.vector.memset(page[:, 0 : T // 2 - 1], 0.0)
+            nc.vector.memset(page[:, T // 2 - 1 : T], 0.0)
+
+        def clear_late_page():
+            page = sb("page%d" % len(pages), T, F32)
+            pages.append(page)
+            for c0 in range(0, T, T // 4):
+                nc.gpsimd.memset(page[:, c0 : c0 + T // 4], 0.0)
 
         def load_rows(name, src, a, c0, w):
             raw = sb(name, 4 * w, F32)
             nc.sync.dma_start(
-                out=raw[:].rearrange("p (j c) -> p j c", j=4),
-                in_=src[512 * a : 512 * (a + 1), c0 : c0 + w].rearrange("(p j) c -> p j c", j=4),
+                out=raw[:].rearrange("p (t c) -> p t c", t=4),
+                in_=src[PASS * a : PASS * (a + 1), c0 : c0 + w].rearrange("(p t) c -> p t c", t=4),
             )
             return raw
 
-        def load_w4(name, r0, r1):
-            words = sb(name, 512 * (r1 - r0), U8)
+        def load_x(c):
+            return [load_rows("x_raw%d%d" % (c, a), x, a, CHUNK * c, CHUNK) for a in range(2)]
+
+        def load_up(r0, r1):
+            return load_rows("up_raw%d" % r0, up, 0, P * r0, P * (r1 - r0))
+
+        def load_w4(r0, r1):
+            words = sb("w4_words%d" % r0, 4 * P * (r1 - r0), U8)
             nc.sync.dma_start(
                 out=words[:].bitcast(I32).rearrange("p (a n) -> p a n", a=2),
-                in_=w4_words[:, :, 256 * r0 : 256 * r1].bitcast(I32).rearrange("a p n -> p a n"),
+                in_=w4_words[:, :, 2 * P * r0 : 2 * P * r1].bitcast(I32).rearrange("a p n -> p a n"),
             )
             return words
 
-        def load_x(c, a):
-            return load_rows("x_raw%d%d" % (c, a), x, a, CHUNK * c, CHUNK)
-
-        d_raw = []
-        x_raw = [[] for c in range(CHUNKS)]
+        down_raw, x_first = [], []
         for a in range(2):
-            d_raw.append(load_rows("d_raw%d" % a, down, a, 0, R))
-            x_raw[0].append(load_x(0, a))
-        upa_raw = load_rows("upa_raw", up, 0, 0, 2 * P)
-        w4_lo = load_w4("w4_lo", 0, PAGES)
-        wg = sb("wg", S, F32)
-        nc.sync.dma_start(out=wg[:, 0:CHUNK], in_=wgo[:, 0:CHUNK])
+            down_raw.append(load_rows("down_raw%d" % a, down, a, 0, R))
+            x_first.append(load_rows("x_raw0%d" % a, x, a, 0, CHUNK))
+        up_raw = {0: load_up(0, 2)}
+        w4_tiles = [load_w4(0, W4_FIRST)]
+        weights = sb("weights", S, F32)
+        nc.sync.dma_start(out=weights[:, 0:CHUNK], in_=wgo[:, 0:CHUNK])
         offsets = keep.tile([P, S // 16], U16, name="offsets")
         nc.sync.dma_start(offsets[:], offs)
-        upb_raw = load_rows("upb_raw", up, 0, 2 * P, (PAGES - 2) * P)
-        for c in range(1, CHUNKS):
-            for a in range(2):
-                x_raw[c].append(load_x(c, a))
-            if c == 1:
-                nc.sync.dma_start(out=wg[:, CHUNK:S], in_=wgo[:, CHUNK:S])
-        upc_raw = load_rows("upc_raw", up, 0, PAGES * P, M - PAGES * P)
-        w4_hi = load_w4("w4_hi", PAGES, ROW_TILES)
+        up_raw[2] = load_up(2, 4)
+        x_raw = [x_first, load_x(1)]
+        up_raw[4] = load_up(4, PAGES)
+        w4_tiles.append(load_w4(W4_FIRST, ROW_TILES))
+        nc.sync.dma_start(out=weights[:, CHUNK:S], in_=wgo[:, CHUNK:S])
+        x_raw.extend(load_x(c) for c in range(2, CHUNKS))
+        up_raw[PAGES] = load_up(PAGES, ROW_TILES)
 
-        def rows4(raw, c0, w):
-            return raw[:].rearrange("p (j c) -> p j c", j=4)[:, :, c0 : c0 + w]
+        def rows4(raw, c0):
+            return raw[:].rearrange("p (t c) -> p t c", t=4)[:, :, c0 : c0 + P]
 
-        b_ps = yps.tile([P, 512], F32, name="y_ps", tag="y_ps")
-        nc.tensor.transpose(b_ps[:, 0:P], b_rows[:], ident[:])
+        b_bank = y_psum.tile([P, BANK], F32, name="y_bank")
+        nc.tensor.transpose(b_bank[:, 0:P], b_rows[:], ident[:])
         b_col = sb("b_col", ROW_TILES, F32)
-        nc.scalar.activation(out=b_col[:], in_=b_ps[:, 0:ROW_TILES], func=IDENTITY)
+        nc.scalar.activation(out=b_col[:], in_=b_bank[:, 0:ROW_TILES], func=IDENTITY)
 
-        d_codes = [sb("d_codes%d" % a, R, U32) for a in range(2)]
-        d_sc = [sb("d_sc%d" % a, R, U8) for a in range(2)]
+        down_codes = [sb("down_codes%d" % a, R, U32) for a in range(2)]
+        down_sc = [sb("down_sc%d" % a, R, U8) for a in range(2)]
         up_codes = sb("up_codes", M, U32)
         up_sc = sb("up_sc", M, U8)
         x_codes = [sb("x_codes%d" % a, S, U32) for a in range(2)]
@@ -119,83 +128,85 @@ def tile_list_hscat_l_bias_kernel(tc, x, w4_words, w4_scales, down, up, b, wgo, 
         h_codes = sb("h_codes", S, U32)
         h_sc = x_sc[1][4:P, CHUNK : S + CHUNK]
 
-        def down_pass(a):
-            raw = d_raw[a][:].rearrange("p (j m t) -> p m j t", j=4, t=4)
-            for half, copy in enumerate((nc.vector.tensor_copy, nc.scalar.copy)):
-                rounded = sb("d_bf%d%d" % (a, half), 1024, BF16)
+        head_copies = (nc.vector.tensor_copy, nc.scalar.copy)
+
+        def quantize_down(a):
+            raw = down_raw[a][:].rearrange("p (j m t) -> p m j t", j=4, t=4)
+            for half, copy in enumerate(head_copies):
+                rounded = sb("down_bf%d%d" % (a, half), 2 * PASS, BF16)
                 copy(
                     out=rounded[:].rearrange("p (t m j) -> p m j t", t=2, j=4),
                     in_=raw[:, :, :, 2 * half : 2 * half + 2],
                 )
-                cols = slice(256 * half, 256 * (half + 1))
-                quantize(d_codes[a][:, cols], d_sc[a][:, cols], rounded[:])
+                cols = slice(2 * P * half, 2 * P * (half + 1))
+                quantize(down_codes[a][:, cols], down_sc[a][:, cols], rounded[:])
 
-        def x0_pass(a):
-            for half, copy in enumerate((nc.vector.tensor_copy, nc.scalar.copy)):
-                rounded = sb("x0_bf%d%d" % (a, half), 512, BF16)
-                weave(copy, rounded[:], rows4(x_raw[0][a], P * half, P))
+        def quantize_first_x(a):
+            for half, copy in enumerate(head_copies):
+                rounded = sb("x_bf0%d%d" % (a, half), PASS, BF16)
+                weave(copy, rounded[:], rows4(x_raw[0][a], P * half))
                 cols = slice(P * half, P * (half + 1))
                 quantize(x_codes[a][:, cols], x_sc[a][:, cols], rounded[:])
 
-        def scalar_weave(name, raw, w):
-            rounded = sb(name, 4 * w, BF16)
+        def round_on_scalar(name, raw, w, tag=None):
+            rounded = sb(name, 4 * w, BF16, tag)
             for c0 in range(0, w, P):
-                weave(nc.scalar.copy, rounded[:, 4 * c0 : 4 * (c0 + P)], rows4(raw, c0, P))
+                weave(nc.scalar.copy, rounded[:, 4 * c0 : 4 * (c0 + P)], rows4(raw, c0))
             return rounded
 
-        def up_rows(name, raw, r0, r1):
-            rounded = scalar_weave(name, raw, P * (r1 - r0))
-            for i0, i1 in ((0, 2), (2, 3)):
-                cols = slice(P * (r0 + i0), P * (r0 + i1))
-                quantize(up_codes[:, cols], up_sc[:, cols], rounded[:, 512 * i0 : 512 * i1])
+        def quantize_up(r0, r1, tag=None):
+            rounded = round_on_scalar("up_bf%d" % r0, up_raw[r0], P * (r1 - r0), tag)
+            for r in range(r0, r1, 2):
+                end = min(r + 2, r1)
+                cols = slice(P * r, P * end)
+                quantize(up_codes[:, cols], up_sc[:, cols], rounded[:, PASS * (r - r0) : PASS * (end - r0)])
+
+        def new_h_banks():
+            return [h_psum.tile([P, BANK], F32, name="h_bank") for half in range(CHUNK // P)]
 
         def h_pass(c, a, banks):
-            for i, bank in enumerate(banks):
-                cols = slice(CHUNK * c + P * i, CHUNK * c + P * (i + 1))
+            for half, bank in enumerate(banks):
+                cols = slice(CHUNK * c + P * half, CHUNK * c + P * (half + 1))
                 for t in range(4):
-                    m_cols = slice(P * t, P * (t + 1))
+                    r_cols = slice(P * t, P * (t + 1))
                     nc.tensor.matmul_mx(
-                        out=bank[:, m_cols],
-                        lhsT=d_codes[a][:, m_cols].bitcast(FP8X4),
-                        lhsT_scale=d_sc[a][:, m_cols],
+                        out=bank[:, r_cols],
+                        lhsT=down_codes[a][:, r_cols].bitcast(FP8X4),
+                        lhsT_scale=down_sc[a][:, r_cols],
                         rhs=x_codes[a][:, cols].bitcast(FP8X4),
                         rhs_scale=x_sc[a][:, cols],
                         start=(a == 0 and t == 0),
                         stop=(a == 1 and t == 3),
                     )
 
-        def h_banks():
-            return [hps.tile([P, 512], F32, name="h_ps", tag="h_ps") for i in range(CHUNK // P)]
-
-        def h_out(copy, rounded, i, bank):
+        def round_h(copy, rounded, half, bank):
             copy(
-                out=rounded[:, 512 * i : 512 * (i + 1)].rearrange("p (n t) -> p n t", t=4),
+                out=rounded[:, PASS * half : PASS * (half + 1)].rearrange("p (n t) -> p n t", t=4),
                 in_=bank[:].rearrange("p (t n) -> p n t", t=4),
             )
 
         def y_sum(r, c0, w):
-            n = P if w < 512 else w
-            bank = yps.tile([P, 512], F32, name="y_ps", tag="y_ps")
-            words, i, count = (w4_lo, r, PAGES) if r < PAGES else (w4_hi, r - PAGES, ROW_TILES - PAGES)
+            step = BANK if w == BANK else P
+            bank = y_psum.tile([P, BANK], F32, name="y_bank")
             for a in range(2):
-                w0 = 256 * (count * a + i)
+                w0 = 2 * P * (W4_FIRST * a + r % W4_FIRST)
                 s0 = M * a + P * r
-                for j in range(0, w, n):
-                    cols = slice(c0 + j, c0 + j + n)
+                for j in range(0, w, step):
+                    cols = slice(c0 + j, c0 + j + step)
                     nc.tensor.matmul_mx(
-                        out=bank[:, j : j + n],
-                        lhsT=words[:, w0 : w0 + 256].bitcast(FP4X4),
+                        out=bank[:, j : j + step],
+                        lhsT=w4_tiles[r // W4_FIRST][:, w0 : w0 + 2 * P].bitcast(FP4X4),
                         lhsT_scale=w4_sc[:, s0 : s0 + P],
                         rhs=x_codes[a][:, cols].bitcast(FP8X4),
                         rhs_scale=x_sc[a][:, cols],
                         start=(a == 0 and j == 0),
                         stop=False,
                     )
-            m_cols = slice(P * r, P * (r + 1))
+            n_cols = slice(P * r, P * (r + 1))
             nc.tensor.matmul_mx(
                 out=bank[:, 0:w],
-                lhsT=up_codes[:, m_cols].bitcast(FP8X4),
-                lhsT_scale=up_sc[:, m_cols],
+                lhsT=up_codes[:, n_cols].bitcast(FP8X4),
+                lhsT_scale=up_sc[:, n_cols],
                 rhs=h_codes[:, c0 : c0 + w].bitcast(FP8X4),
                 rhs_scale=h_sc[:, c0 : c0 + w],
                 start=False,
@@ -203,79 +214,86 @@ def tile_list_hscat_l_bias_kernel(tc, x, w4_words, w4_scales, down, up, b, wgo, 
             )
             return bank[:, 0:w]
 
-        def add_bias(r, staged, bank):
-            nc.scalar.activation(out=staged, in_=bank, func=IDENTITY, bias=b_col[:, r : r + 1])
+        def add_bias(r, staged, sums):
+            nc.scalar.activation(out=staged, in_=sums, func=IDENTITY, bias=b_col[:, r : r + 1])
 
         def scatter(r, c0, w, staged):
             page = pages[r % PAGES]
             nc.vector.tensor_tensor(
-                page[:].indirect(offsets[:, c0 // 16 : (c0 + w) // 16]), staged, wg[:, c0 : c0 + w], MULT
+                page[:].indirect(offsets[:, c0 // 16 : (c0 + w) // 16]), staged, weights[:, c0 : c0 + w], MULT
             )
             if c0 + w == S:
                 nc.sync.dma_start(out=out[P * r : P * (r + 1), :], in_=page[:])
 
-        def place(c, r, bank, staged):
-            add_bias(r, staged, bank)
-            scatter(r, CHUNK * c, CHUNK, staged)
+        def place(r, c0, sums, staged):
+            add_bias(r, staged, sums)
+            scatter(r, c0, CHUNK, staged)
 
-        def last(raw, w, i):
-            return raw[:, w * (i + 1) - CHUNK : w * (i + 1)]
+        staging = sb("staging", 3 * S, F32)
 
-        staging = sb("staging", 3 * CHUNKS * CHUNK, F32)
-
-        def free(c, i):
+        def own_range(c, i):
             return staging[:, CHUNK * (3 * c + i) : CHUNK * (3 * c + i + 1)]
 
-        banks = h_banks()
+        def row_end(raw, t):
+            end = raw.shape[1] // 4 * (t + 1)
+            return raw[:, end - CHUNK : end]
+
+        banks = new_h_banks()
         for a in range(2):
-            down_pass(a)
-            x0_pass(a)
+            quantize_down(a)
+            quantize_first_x(a)
             h_pass(0, a, banks)
-        h_bf = sb("h_bf0", 1024, BF16)
-        upa_bf = sb("upa_bf", 1024, BF16)
-        for half, copy in enumerate((nc.vector.tensor_copy, nc.scalar.copy)):
+        h_bf = sb("h_bf0", 2 * PASS, BF16, "page2")
+        up_bf = sb("up_bf0", 2 * PASS, BF16)
+        for half, copy in enumerate(head_copies):
             cols = slice(P * half, P * (half + 1))
-            wide = slice(512 * half, 512 * (half + 1))
-            h_out(copy, h_bf, half, banks[half])
+            wide = slice(PASS * half, PASS * (half + 1))
+            round_h(copy, h_bf, half, banks[half])
             quantize(h_codes[:, cols], h_sc[:, cols], h_bf[:, wide])
-            weave(copy, upa_bf[:, wide], rows4(upa_raw, P * half, P))
-            quantize(up_codes[:, cols], up_sc[:, cols], upa_bf[:, wide])
-            add_bias(0, free(0, 0)[:, cols], y_sum(0, P * half, P))
-            scatter(0, P * half, P, free(0, 0)[:, cols])
-        for r in range(3, PAGES):
-            for half in range(2):
-                nc.vector.memset(pages[r][:, 1024 * half : 1024 * (half + 1)], 0.0)
+            weave(copy, up_bf[:, wide], rows4(up_raw[0], P * half))
+            quantize(up_codes[:, cols], up_sc[:, cols], up_bf[:, wide])
+            add_bias(0, own_range(0, 0)[:, cols], y_sum(0, P * half, P))
+            scatter(0, P * half, P, own_range(0, 0)[:, cols])
+        clear_late_page()
 
         for c in range(CHUNKS):
             c0 = CHUNK * c
             if c == 0:
-                up_rows("upb_bf", upb_raw, 2, PAGES)
+                quantize_up(2, 4, "page3")
+                clear_late_page()
+                place(1, c0, y_sum(1, c0, CHUNK), row_end(up_raw[2], 0))
             else:
-                place(c, 0, y_sum(0, c0, CHUNK), free(c, 0))
-            place(c, 1, y_sum(1, c0, CHUNK), last(upb_raw, 3 * P, 0) if c == 0 else free(c, 1))
-            held = [y_sum(r, c0, CHUNK) for r in (2, 3)]
-            if c + 1 < CHUNKS:
+                for r in range(2):
+                    place(r, c0, y_sum(r, c0, CHUNK), own_range(c, r))
+            sums = [y_sum(r, c0, CHUNK) for r in (2, 3)]
+            if c + 1 == CHUNKS:
+                quantize_up(PAGES, ROW_TILES)
+                for i in range(2):
+                    place(2 + i, c0, sums[i], row_end(up_raw[PAGES], i))
+            else:
                 cols = slice(c0 + CHUNK, c0 + 2 * CHUNK)
-                banks = h_banks()
+                banks = new_h_banks()
                 for a in range(2):
-                    x_bf = scalar_weave("x_bf%d%d" % (c + 1, a), x_raw[c + 1][a], CHUNK)
+                    tag = "page4" if (c, a) == (0, 1) else None
+                    x_bf = round_on_scalar("x_bf%d%d" % (c + 1, a), x_raw[c + 1][a], CHUNK, tag)
                     quantize(x_codes[a][:, cols], x_sc[a][:, cols], x_bf[:])
                     h_pass(c + 1, a, banks)
-                for i in range(2):
-                    place(c, 2 + i, held[i], last(x_raw[c + 1][1], CHUNK, i))
-                h_bf = sb("h_bf%d" % (c + 1), 1024, BF16)
-                for i in range(2):
-                    h_out(nc.scalar.copy, h_bf, i, banks[i])
+                place(2, c0, sums[0], row_end(x_raw[c + 1][1], 0))
+                if c == 0:
+                    clear_late_page()
+                    quantize_up(4, PAGES)
+                    place(3, c0, sums[1], row_end(up_raw[4], 1))
+                else:
+                    place(3, c0, sums[1], row_end(x_raw[c + 1][1], 1))
+                h_bf = sb("h_bf%d" % (c + 1), 2 * PASS, BF16)
+                for half in range(2):
+                    round_h(nc.scalar.copy, h_bf, half, banks[half])
                 quantize(h_codes[:, cols], h_sc[:, cols], h_bf[:])
-            else:
-                up_rows("upc_bf", upc_raw, PAGES, ROW_TILES)
-                for i in range(2):
-                    place(c, 2 + i, held[i], last(upc_raw, 3 * P, i))
-            place(c, 4, y_sum(4, c0, CHUNK), free(c, 2))
+            place(4, c0, y_sum(4, c0, CHUNK), own_range(c, 2))
 
-        spare = [d_raw[0][:, 0:S], d_raw[0][:, S : 2 * S], d_raw[1][:, 0:S]]
+        whole = [down_raw[0][:, 0:S], down_raw[0][:, S : 2 * S], down_raw[1][:, 0:S]]
         for r in range(PAGES, ROW_TILES):
-            staged = spare[r - PAGES]
-            for c0 in range(0, S, 512):
-                add_bias(r, staged[:, c0 : c0 + 512], y_sum(r, c0, 512))
+            staged = whole[r - PAGES]
+            for c0 in range(0, S, BANK):
+                add_bias(r, staged[:, c0 : c0 + BANK], y_sum(r, c0, BANK))
             scatter(r, 0, S, staged)

from contextlib import ExitStack

import concourse.mybir as mybir
from concourse.masks import make_identity

K, M, T, S, R = 1024, 1024, 2048, 1024, 512
FLOPS = 2 * S * (K * R + K * M + R * M)

F32 = mybir.dt.float32
BF16 = mybir.dt.bfloat16
I32 = mybir.dt.int32
U32 = mybir.dt.uint32
U16 = mybir.dt.uint16
U8 = mybir.dt.uint8
FP8X4 = mybir.dt.float8_e4m3fn_x4
FP4X4 = mybir.dt.float4_e2m1fn_x4
IDENTITY = mybir.ActivationFunctionType.Identity
MULT = mybir.AluOpType.mult

P = 128
PASS = 4 * P
BANK = 512
ROW_TILES = M // P
CHUNK = 256
CHUNKS = S // CHUNK
PAGES = 5
W4_FIRST = 4


def weave(copy, dst, src):
    copy(
        out=dst.rearrange("p (c i t) -> p c t i", i=4, t=4),
        in_=src.rearrange("p t (c i) -> p c t i", i=4),
    )


def tile_list_hscat_l_bias_kernel(tc, x, w4_words, w4_scales, down, up, b, wgo, offs, out):
    nc = tc.nc
    with ExitStack() as ctx:
        keep = ctx.enter_context(tc.tile_pool(name="keep", bufs=1))
        h_psum = ctx.enter_context(tc.psum_pool(name="h_psum", bufs=4))
        y_psum = ctx.enter_context(tc.psum_pool(name="y_psum", bufs=4))

        def sb(name, width, dtype, tag=None):
            return keep.tile([P, width], dtype, name=name, tag=tag or name, align_bytes=64)

        def quantize(codes, scales, values):
            nc.vector.quantize_mx(out=codes.bitcast(FP8X4), scales=scales, in_=values)

        b_rows = sb("b_rows", P, F32)
        nc.gpsimd.memset(b_rows[:], 0.0)
        nc.gpsimd.dma_start(out=b_rows[0:ROW_TILES, :], in_=b.rearrange("(i p) -> i p", p=P))
        ident = sb("ident", P, F32)
        make_identity(nc, ident[:])
        w4_sc = sb("w4_sc", 2 * M, U8)
        nc.vector.memset(w4_sc[:].bitcast(I32), 0)
        for q in range(4):
            nc.gpsimd.dma_start(
                out=w4_sc[32 * q : 32 * q + 4, :].bitcast(I32).rearrange("r (a n) -> r a n", a=2),
                in_=w4_scales[:, 4 * q : 4 * q + 4, :].bitcast(I32).rearrange("a r n -> r a n"),
            )

        pages = [sb("page%d" % r, T, F32) for r in range(2)]
        for page in pages:
            nc.vector.memset(page[:, 0 : T // 2 - 1], 0.0)
            nc.vector.memset(page[:, T // 2 - 1 : T], 0.0)

        def clear_late_page():
            page = sb("page%d" % len(pages), T, F32)
            pages.append(page)
            for c0 in range(0, T, T // 4):
                nc.gpsimd.memset(page[:, c0 : c0 + T // 4], 0.0)

        def load_rows(name, src, a, c0, w):
            raw = sb(name, 4 * w, F32)
            nc.sync.dma_start(
                out=raw[:].rearrange("p (t c) -> p t c", t=4),
                in_=src[PASS * a : PASS * (a + 1), c0 : c0 + w].rearrange("(p t) c -> p t c", t=4),
            )
            return raw

        def load_x(c):
            return [load_rows("x_raw%d%d" % (c, a), x, a, CHUNK * c, CHUNK) for a in range(2)]

        def load_up(r0, r1):
            return load_rows("up_raw%d" % r0, up, 0, P * r0, P * (r1 - r0))

        def load_w4(r0, r1):
            words = sb("w4_words%d" % r0, 4 * P * (r1 - r0), U8)
            nc.sync.dma_start(
                out=words[:].bitcast(I32).rearrange("p (a n) -> p a n", a=2),
                in_=w4_words[:, :, 2 * P * r0 : 2 * P * r1].bitcast(I32).rearrange("a p n -> p a n"),
            )
            return words

        down_raw, x_first = [], []
        for a in range(2):
            down_raw.append(load_rows("down_raw%d" % a, down, a, 0, R))
            x_first.append(load_rows("x_raw0%d" % a, x, a, 0, CHUNK))
        up_raw = {0: load_up(0, 2)}
        w4_tiles = [load_w4(0, W4_FIRST)]
        weights = sb("weights", S, F32)
        nc.sync.dma_start(out=weights[:, 0:CHUNK], in_=wgo[:, 0:CHUNK])
        offsets = keep.tile([P, S // 16], U16, name="offsets")
        nc.sync.dma_start(offsets[:], offs)
        up_raw[2] = load_up(2, 4)
        x_raw = [x_first, load_x(1)]
        up_raw[4] = load_up(4, PAGES)
        w4_tiles.append(load_w4(W4_FIRST, ROW_TILES))
        nc.sync.dma_start(out=weights[:, CHUNK:S], in_=wgo[:, CHUNK:S])
        x_raw.extend(load_x(c) for c in range(2, CHUNKS))
        up_raw[PAGES] = load_up(PAGES, ROW_TILES)

        def rows4(raw, c0):
            return raw[:].rearrange("p (t c) -> p t c", t=4)[:, :, c0 : c0 + P]

        b_bank = y_psum.tile([P, BANK], F32, name="y_bank")
        nc.tensor.transpose(b_bank[:, 0:P], b_rows[:], ident[:])
        b_col = sb("b_col", ROW_TILES, F32)
        nc.scalar.activation(out=b_col[:], in_=b_bank[:, 0:ROW_TILES], func=IDENTITY)

        down_codes = [sb("down_codes%d" % a, R, U32) for a in range(2)]
        down_sc = [sb("down_sc%d" % a, R, U8) for a in range(2)]
        up_codes = sb("up_codes", M, U32)
        up_sc = sb("up_sc", M, U8)
        x_codes = [sb("x_codes%d" % a, S, U32) for a in range(2)]
        x_sc = [sb("x_sc0", S, U8), sb("x_sc1", S + CHUNK, U8)]
        h_codes = sb("h_codes", S, U32)
        h_sc = x_sc[1][4:P, CHUNK : S + CHUNK]

        head_copies = (nc.vector.tensor_copy, nc.scalar.copy)

        def quantize_down(a):
            raw = down_raw[a][:].rearrange("p (j m t) -> p m j t", j=4, t=4)
            for half, copy in enumerate(head_copies):
                rounded = sb("down_bf%d%d" % (a, half), 2 * PASS, BF16)
                copy(
                    out=rounded[:].rearrange("p (t m j) -> p m j t", t=2, j=4),
                    in_=raw[:, :, :, 2 * half : 2 * half + 2],
                )
                cols = slice(2 * P * half, 2 * P * (half + 1))
                quantize(down_codes[a][:, cols], down_sc[a][:, cols], rounded[:])

        def quantize_first_x(a):
            for half, copy in enumerate(head_copies):
                rounded = sb("x_bf0%d%d" % (a, half), PASS, BF16)
                weave(copy, rounded[:], rows4(x_raw[0][a], P * half))
                cols = slice(P * half, P * (half + 1))
                quantize(x_codes[a][:, cols], x_sc[a][:, cols], rounded[:])

        def round_on_scalar(name, raw, w, tag=None):
            rounded = sb(name, 4 * w, BF16, tag)
            for c0 in range(0, w, P):
                weave(nc.scalar.copy, rounded[:, 4 * c0 : 4 * (c0 + P)], rows4(raw, c0))
            return rounded

        def quantize_up(r0, r1, tag=None):
            rounded = round_on_scalar("up_bf%d" % r0, up_raw[r0], P * (r1 - r0), tag)
            for r in range(r0, r1, 2):
                end = min(r + 2, r1)
                cols = slice(P * r, P * end)
                quantize(up_codes[:, cols], up_sc[:, cols], rounded[:, PASS * (r - r0) : PASS * (end - r0)])

        def new_h_banks():
            return [h_psum.tile([P, BANK], F32, name="h_bank") for half in range(CHUNK // P)]

        def h_pass(c, a, banks):
            for half, bank in enumerate(banks):
                cols = slice(CHUNK * c + P * half, CHUNK * c + P * (half + 1))
                for t in range(4):
                    r_cols = slice(P * t, P * (t + 1))
                    nc.tensor.matmul_mx(
                        out=bank[:, r_cols],
                        lhsT=down_codes[a][:, r_cols].bitcast(FP8X4),
                        lhsT_scale=down_sc[a][:, r_cols],
                        rhs=x_codes[a][:, cols].bitcast(FP8X4),
                        rhs_scale=x_sc[a][:, cols],
                        start=(a == 0 and t == 0),
                        stop=(a == 1 and t == 3),
                    )

        def round_h(copy, rounded, half, bank):
            copy(
                out=rounded[:, PASS * half : PASS * (half + 1)].rearrange("p (n t) -> p n t", t=4),
                in_=bank[:].rearrange("p (t n) -> p n t", t=4),
            )

        def y_sum(r, c0, w):
            step = BANK if w == BANK else P
            bank = y_psum.tile([P, BANK], F32, name="y_bank")
            for a in range(2):
                w0 = 2 * P * (W4_FIRST * a + r % W4_FIRST)
                s0 = M * a + P * r
                for j in range(0, w, step):
                    cols = slice(c0 + j, c0 + j + step)
                    nc.tensor.matmul_mx(
                        out=bank[:, j : j + step],
                        lhsT=w4_tiles[r // W4_FIRST][:, w0 : w0 + 2 * P].bitcast(FP4X4),
                        lhsT_scale=w4_sc[:, s0 : s0 + P],
                        rhs=x_codes[a][:, cols].bitcast(FP8X4),
                        rhs_scale=x_sc[a][:, cols],
                        start=(a == 0 and j == 0),
                        stop=False,
                    )
            n_cols = slice(P * r, P * (r + 1))
            nc.tensor.matmul_mx(
                out=bank[:, 0:w],
                lhsT=up_codes[:, n_cols].bitcast(FP8X4),
                lhsT_scale=up_sc[:, n_cols],
                rhs=h_codes[:, c0 : c0 + w].bitcast(FP8X4),
                rhs_scale=h_sc[:, c0 : c0 + w],
                start=False,
                stop=True,
            )
            return bank[:, 0:w]

        def add_bias(r, staged, sums):
            nc.scalar.activation(out=staged, in_=sums, func=IDENTITY, bias=b_col[:, r : r + 1])

        def scatter(r, c0, w, staged):
            page = pages[r % PAGES]
            nc.vector.tensor_tensor(
                page[:].indirect(offsets[:, c0 // 16 : (c0 + w) // 16]), staged, weights[:, c0 : c0 + w], MULT
            )
            if c0 + w == S:
                nc.sync.dma_start(out=out[P * r : P * (r + 1), :], in_=page[:])

        def place(r, c0, sums, staged):
            add_bias(r, staged, sums)
            scatter(r, c0, CHUNK, staged)

        staging = sb("staging", 3 * S, F32)

        def own_range(c, i):
            return staging[:, CHUNK * (3 * c + i) : CHUNK * (3 * c + i + 1)]

        def row_end(raw, t):
            end = raw.shape[1] // 4 * (t + 1)
            return raw[:, end - CHUNK : end]

        banks = new_h_banks()
        for a in range(2):
            quantize_down(a)
            quantize_first_x(a)
            h_pass(0, a, banks)
        h_bf = sb("h_bf0", 2 * PASS, BF16, "page2")
        up_bf = sb("up_bf0", 2 * PASS, BF16)
        for half, copy in enumerate(head_copies):
            cols = slice(P * half, P * (half + 1))
            wide = slice(PASS * half, PASS * (half + 1))
            round_h(copy, h_bf, half, banks[half])
            quantize(h_codes[:, cols], h_sc[:, cols], h_bf[:, wide])
            weave(copy, up_bf[:, wide], rows4(up_raw[0], P * half))
            quantize(up_codes[:, cols], up_sc[:, cols], up_bf[:, wide])
            add_bias(0, own_range(0, 0)[:, cols], y_sum(0, P * half, P))
            scatter(0, P * half, P, own_range(0, 0)[:, cols])
        clear_late_page()

        for c in range(CHUNKS):
            c0 = CHUNK * c
            if c == 0:
                quantize_up(2, 4, "page3")
                clear_late_page()
                place(1, c0, y_sum(1, c0, CHUNK), row_end(up_raw[2], 0))
            else:
                for r in range(2):
                    place(r, c0, y_sum(r, c0, CHUNK), own_range(c, r))
            sums = [y_sum(r, c0, CHUNK) for r in (2, 3)]
            if c + 1 == CHUNKS:
                quantize_up(PAGES, ROW_TILES)
                for i in range(2):
                    place(2 + i, c0, sums[i], row_end(up_raw[PAGES], i))
            else:
                cols = slice(c0 + CHUNK, c0 + 2 * CHUNK)
                banks = new_h_banks()
                for a in range(2):
                    tag = "page4" if (c, a) == (0, 1) else None
                    x_bf = round_on_scalar("x_bf%d%d" % (c + 1, a), x_raw[c + 1][a], CHUNK, tag)
                    quantize(x_codes[a][:, cols], x_sc[a][:, cols], x_bf[:])
                    h_pass(c + 1, a, banks)
                place(2, c0, sums[0], row_end(x_raw[c + 1][1], 0))
                if c == 0:
                    clear_late_page()
                    quantize_up(4, PAGES)
                    place(3, c0, sums[1], row_end(up_raw[4], 1))
                else:
                    place(3, c0, sums[1], row_end(x_raw[c + 1][1], 1))
                h_bf = sb("h_bf%d" % (c + 1), 2 * PASS, BF16)
                for half in range(2):
                    round_h(nc.scalar.copy, h_bf, half, banks[half])
                quantize(h_codes[:, cols], h_sc[:, cols], h_bf[:])
            place(4, c0, y_sum(4, c0, CHUNK), own_range(c, 2))

        whole = [down_raw[0][:, 0:S], down_raw[0][:, S : 2 * S], down_raw[1][:, 0:S]]
        for r in range(PAGES, ROW_TILES):
            staged = whole[r - PAGES]
            for c0 in range(0, S, BANK):
                add_bias(r, staged[:, c0 : c0 + BANK], y_sum(r, c0, BANK))
            scatter(r, 0, S, staged)
